import numpy as np
CORES = [36,38,116,118,124,126,164,166,244,246,252,254]
N = 12
T = 1024
def entries(a): return a.T.reshape(-1)
def pack(v, P): return np.ascontiguousarray(np.asarray(v, np.int32).reshape(-1, P).T)
def lists(rng, how):
    h = rng.integers(0, N * T, 8)
    if how == "zero": h[:] = 0
    if how == "blocks": h = T * rng.integers(1, N, 8)
    if how == "last": h[:] = N * T - 1
    if how == "mixed": h = T * rng.choice([q for q in range(N) if q & (q - 1)], 8) + rng.integers(1, T, 8)
    if how == "small": h = rng.integers(1, T, 8)
    h[1:] = 0
    return {"hh": np.broadcast_to(pack(np.concatenate([h, np.zeros(24, np.int64)]), 16), (N, 16, 2)).copy()}
def setup_inputs(rng):
    return dict({"x": rng.standard_normal((N, 128, T), dtype=np.float32)}, **lists(rng, "uniform"))
def setup_inputs_blocks(rng):
    d = setup_inputs(rng); d.update(lists(rng, "blocks"))
    for k in ("x",): d[k] = (d[k].astype(np.float32) * 1048576.0).astype(d[k].dtype)
    return d
def setup_inputs_last(rng):
    d = setup_inputs(rng); d.update(lists(rng, "last"))
    for k in ("x",): d[k] = (d[k].astype(np.float32) * (1 / 1024.0)).astype(d[k].dtype)
    return d
def setup_inputs_mixed(rng):
    d = setup_inputs(rng); d.update(lists(rng, "mixed"))
    return d
def setup_inputs_small(rng):
    d = setup_inputs(rng); d.update(lists(rng, "small"))
    return d
def setup_inputs_zero(rng):
    d = setup_inputs(rng); d.update(lists(rng, "zero"))
    return d
def check_inputs(x):
    bad = []
    if x["hh"].min() < 0 or x["hh"].max() >= N * T: bad.append("hh out of range")
    if entries(x["hh"][0])[1:].any(): bad.append("an entry that should be 0 isn't")
    if not all(np.array_equal(a, x["hh"][0]) for a in x["hh"]): bad.append("hh isn't alike on all ranks")
    return bad
def reference(x, hh):
    h = entries(hh[0]); A = np.concatenate(list(x), axis=1)
    Y = np.roll(A, -int(h[0]), axis=1)
    return {"y": np.stack([Y[:, T * r:T * r + T] for r in range(N)])}

@@ -1,0 +1,291 @@
+from concourse.bass import DstId, RemoteDMATransfer
+from concourse.mybir import AluOpType, ActivationFunctionType
+
+WORLD = 256
+N = 12
+COLS = 1024
+PW = 128
+ADD = AluOpType.add
+
+SCRATCH = {
+    "hI": ("sbuf", [16, 2], "int32"),
+    "hB": ("sbuf", [128, 2], "int32"),
+    "hF": ("sbuf", [128, 1], "float32"),
+    "pI": ("sbuf", [128, 1], "int32"),
+    "pM": ("sbuf", [128, 1], "int32"),
+    "pF": ("sbuf", [128, 1], "float32"),
+    "k1": ("sbuf", [128, 64], "int32"),
+    "a1": ("sbuf", [128, 64], "int32"),
+    "b1": ("sbuf", [128, 64], "int32"),
+    "l1": ("sbuf", [128, 64], "uint16"),
+    "k2": ("sbuf", [128, 96], "int32"),
+    "c2": ("sbuf", [128, 96], "int32"),
+    "d2": ("sbuf", [128, 96], "int32"),
+    "a2": ("sbuf", [128, 96], "int32"),
+    "m2": ("sbuf", [128, 96], "int32"),
+    "t2": ("sbuf", [128, 96], "int32"),
+    "u2": ("sbuf", [128, 96], "int32"),
+    "w2": ("sbuf", [128, 96], "int32"),
+    "l2": ("sbuf", [128, 96], "uint16"),
+    "xs": ("sbuf", [128, COLS], "float32"),
+    "rot": ("sbuf", [128, COLS], "float32"),
+    "rl": ("sbuf", [128, COLS // 2], "float32"),
+    "ex": ("sbuf", [128, PW + N * PW], "float32"),
+    "s2": ("sbuf", [128, N * PW], "float32"),
+    "land": ("sbuf", [128, COLS], "float32"),
+}
+SEMAPHORES = (["hld", "xld", "hb", "io0", "v", "lst1", "lst2", "hand", "harr", "arr", "own0", "own1", "rly", "lsem", "sty", "stz"]
+              + ["tn%d" % k for k in range(4)] + ["ga%d" % k for k in range(4)] + ["gb%d" % k for k in range(4)]
+              + ["out%d" % k for k in range(4)])
+
+
+def bits(mask):
+    return [e for e in range(16) if (mask >> e) & 1]
+
+
+def part(engines, n, i):
+    w = len(engines) // n
+    m = 0
+    for e in engines[i * w:(i + 1) * w]:
+        m |= 1 << e
+    return m
+
+
+def layout(T, topo):
+    where = lambda c: (topo.host(c), topo.chip(c))
+    chips = []
+    for c in T.cores:
+        if where(c) not in chips:
+            chips.append(where(c))
+    ranks = {q: [c for c in T.cores if where(c) == q] for q in chips}
+    plane = lambda a: [q for q in chips if q == where(a) or topo.same_plane(a, ranks[q][0])]
+    hubs = max((plane(ranks[q][0]) for q in chips), key=len)
+    reach = lambda c: all(topo.may_write(c, d) for d in T.cores if d != c)
+    on_chip = {q: [c for c in range(WORLD) if where(c) == q] for q in chips}
+    L = {"chips": chips, "ranks": ranks, "hubs": hubs, "where": where, "mid": [], "relay": {}}
+    for q in hubs:
+        a = [c for c in ranks[q] if reach(c)][0]
+        b = [c for c in on_chip[q] if reach(c) and topo.die(c) != topo.die(a) and c not in T.cores][0]
+        L["mid"].append((a, b))
+    for q in chips:
+        if q in hubs:
+            continue
+        for c in ranks[q]:
+            if not reach(c):
+                L["relay"][c] = [d for d in on_chip[q] if reach(d) and topo.die(d) != topo.die(c)][:2]
+    far = [c for c in T.cores if where(c) != chips[0]][0]
+    near = on_chip[chips[0]]
+    src = [c for c in near if reach(c)][0]
+    L["off"] = bits(topo.mask(src, far))
+    L["all"] = bits(topo.mask(src, [c for c in near if c != src][0]))
+    L["up"] = [e for e in L["all"] if e not in L["off"]]
+    return L
+
+
+def rank_program(g, core, T, topo):
+    L = layout(T, topo)
+    chip = L["where"](core)
+    rank = T.rank_of(core)
+    mids = [c for pair in L["mid"] for c in pair]
+    relays = [c for pair in L["relay"].values() for c in pair]
+    if rank is None and core not in mids and core not in relays:
+        return
+    S = T.sem
+    off, up, every = L["off"], L["up"], L["all"]
+    hubs, chips, mid = L["hubs"], L["chips"], L["mid"]
+    is_hub = chip in hubs
+    me = hubs.index(chip) if is_hub else None
+    first = 2 * chips.index(chip)
+    sent = [0]
+    vn = [0]
+
+    def xfer(dst, src_ap, dst_ap, sem, mask):
+        rid, pid = topo.addr(dst, core)
+        return RemoteDMATransfer(dst_ids=[DstId(rid=rid, pnc=pid)], dma_engine_mask=mask, remote_sem=sem, src=src_ap, dst=dst_ap)
+
+    def send(transfers, engines):
+        g.remote_dma_fused(transfers, local_sem=S.lsem)
+        sent[0] += engines
+
+    def vec(call, *args):
+        if vn[0]:
+            g.vector.wait_ge(S.v, vn[0])
+        call(*args).then_inc(S.v, 1)
+        vn[0] += 1
+
+    def slot(dst_chip, r):
+        a = PW + PW * ((r - 2 * chips.index(dst_chip)) % N)
+        return T.ex[:, a:a + PW]
+
+    def gather(on_vector, out, win, lst):
+        if on_vector:
+            return g.vector.tensor_copy(out, win.indirect(lst))
+        return g.scalar.activation(out, win.indirect(lst), ActivationFunctionType.Copy, bias=-0.0)
+
+    def order(m):
+        return [(m + 1 + k) % 4 for k in range(4)] if m is not None else [0, 1, 2, 3]
+
+    if rank is not None:
+        g.sync.dma_start(T.hI[0:1, :], T.hh[0:1, :]).then_inc(S.hld, 16)
+        g.scalar.dma_start(T.xs[:], T.x[:]).then_inc(S.xld, 16)
+    if rank is not None or core in mids:
+        n_io = 1
+        g.iota(T.pI[:], [[0, 1]], 0, 1).then_inc(S.io0, 1)
+        if rank is not None:
+            g.iota(T.k1[:], [[16, 64]], 0, 0).then_inc(S.io0, 1)
+            n_io += 1
+        if core in mids:
+            g.iota(T.k2[:], [[1024, 12], [16, 8]], PW * mids.index(core), 0).then_inc(S.io0, 1)
+            g.iota(T.c2[:], [[0, 12], [16, 8]], 0, 0).then_inc(S.io0, 1)
+            n_io += 2
+        if rank is not None:
+            g.wait_ge(S.hld, 16)
+            g.partition_broadcast(T.hB[:], T.hI[0:1, :], 128).then_inc(S.hb, 1)
+        V = g.vector
+        V.wait_ge(S.io0, n_io)
+        vec(V.tensor_scalar, T.pM[:], T.pI[:], 15, None, AluOpType.bitwise_and)
+        vec(V.tensor_copy, T.pF[:], T.pM[:])
+        if core in mids:
+            vec(V.tensor_scalar, T.d2[:], T.c2[:], T.pF[:], None, ADD)
+        if rank is not None:
+            V.wait_ge(S.hb, 1)
+        else:
+            V.wait_ge(S.harr, len(up))
+        vec(V.tensor_copy, T.hF[:], T.hB[:, 0:1])
+
+    if rank is not None:
+        vec(V.tensor_scalar, T.a1[:], T.k1[:], T.pF[:], T.hF[:], ADD, ADD)
+        vec(V.tensor_scalar, T.b1[:], T.a1[:], COLS - 1, None, AluOpType.bitwise_and)
+        V.wait_ge(S.v, vn[0])
+        V.tensor_copy(T.l1[:], T.b1[:]).then_inc(S.lst1, 1)
+        for q in (V, g.scalar):
+            q.wait_ge(S.lst1, 1)
+            q.wait_ge(S.xld, 16)
+
+        def turn(on_vector, out, a, n):
+            return gather(on_vector, out, T.xs[:], T.l1[:, a // 16:(a + n) // 16])
+
+        for k, m in enumerate(order(me)):
+            a = 2 * PW * m
+            if m == me and core in mids:
+                turn(k % 2 == 0, T.rot[:, a + PW:a + 2 * PW], a + PW, PW).then_inc(S["tn%d" % k], 1)
+                turn(k % 2 == 0, slot(chip, rank), a, PW).then_inc(S.own0, 1)
+            else:
+                turn(k % 2 == 0, T.rot[:, a:a + 2 * PW], a, 2 * PW).then_inc(S["tn%d" % k], 1)
+
+    def pieces(buf, a0, ms, r, n):
+        out = []
+        for m in ms:
+            for j in (0, 1):
+                a = 2 * PW * m + PW * j - a0
+                out.append(xfer(mid[m][j], buf[:, a:a + PW], slot(hubs[m], r), S.arr, part(off, n, len(out))))
+        return out
+
+    if rank is not None:
+        o = order(me)
+        if core in L["relay"]:
+            for k, d in enumerate(L["relay"][core]):
+                g.wait_ge(S["tn%d" % (2 * k)], 1)
+                g.wait_ge(S["tn%d" % (2 * k + 1)], 1)
+                send([xfer(d, T.rot[:, 512 * k:512 * k + 512], T.rl[:], S.rly, part(every, 1, 0))], len(every))
+        else:
+            g.wait_ge(S.tn0, 1)
+            g.wait_ge(S.tn1, 1)
+            send(pieces(T.rot, 0, o[0:2], rank, 4), len(off))
+            g.wait_ge(S.tn2, 1)
+            if is_hub:
+                send(pieces(T.rot, 0, o[2:3], rank, 2), len(off))
+                g.wait_ge(S.tn3, 1)
+                a = 2 * PW * me
+                if core in mids:
+                    send([xfer(mid[me][1], T.rot[:, a + PW:a + 2 * PW], slot(chip, rank), S.arr, part(up, 1, 0))], len(up))
+                else:
+                    send([xfer(mid[me][1], T.rot[:, a:a + 2 * PW], T.ex[:, 0:2 * PW], S.hand, part(up, 1, 0))], len(up))
+                    g.wait_ge(S.hb, 1)
+                    send([xfer(mid[me][1], T.hB[:], T.hB[:], S.harr, part(up, 1, 0))], len(up))
+            else:
+                g.wait_ge(S.tn3, 1)
+                send(pieces(T.rot, 0, o[2:4], rank, 4), len(off))
+    for src, pair in L["relay"].items():
+        if core in pair:
+            k = pair.index(core)
+            g.wait_ge(S.rly, len(every))
+            send(pieces(T.rl, 512 * k, [2 * k, 2 * k + 1], T.rank_of(src), 4), len(off))
+
+    groups = [(range(2, 6), 4), (range(6, 10), 4), (range(10, 12), 2), (range(0, 2), 2)]
+    if core in mids:
+        j = mids.index(core)
+        vec(V.tensor_scalar, T.a2[:], T.k2[:], T.pF[:], T.hF[:], ADD, ADD)
+        vec(V.tensor_scalar, T.m2[:], T.a2[:], 3, 31 * PW, AluOpType.arith_shift_right, AluOpType.bitwise_and)
+        vec(V.tensor_scalar, T.t2[:], T.m2[:], N * PW, -N * PW, AluOpType.is_ge, AluOpType.mult)
+        vec(V.tensor_tensor, T.u2[:], T.m2[:], T.t2[:], ADD)
+        vec(V.tensor_tensor, T.w2[:], T.u2[:], T.d2[:], ADD)
+        V.wait_ge(S.v, vn[0])
+        V.tensor_copy(T.l2[:], T.w2[:]).then_inc(S.lst2, 1)
+
+        expect = 0
+        for c in T.cores:
+            w = L["where"](c)
+            if w == chip:
+                continue
+            k = order(hubs.index(w) if w in hubs else None).index(me)
+            expect += len(off) // (2 if (w in hubs and k == 2) else 4)
+        helper = rank is None
+        expect += len(up) if helper else len(off)
+        if helper:
+            other = [c for c in L["ranks"][chip] if c not in mids][0]
+            g.wait_ge(S.hand, len(up))
+            send([xfer(mid[me][0], T.ex[:, 0:PW], slot(chip, T.rank_of(other)), S.arr, part(off, 1, 0))], len(off))
+        for q in (V, g.scalar):
+            q.wait_ge(S.lst2, 1)
+            if helper:
+                q.wait_ge(S.hand, len(up))
+            else:
+                q.wait_ge(S.own0, 1)
+            q.wait_ge(S.arr, expect)
+
+        def pick(on_vector, d, n, out):
+            return gather(on_vector, out, T.ex[:, PW:PW + N * PW], T.l2[:, 8 * d:8 * (d + n)])
+
+        for k, (ds, n) in enumerate(groups):
+            half = len(ds) // 2
+            for on_vector, d in ((True, ds[0]), (False, ds[half])):
+                if T.cores[(first + d) % N] == core:
+                    pick(on_vector, d, half, T.land[:, PW * j:PW * j + PW]).then_inc(S.own1, 1)
+                else:
+                    pick(on_vector, d, half, T.s2[:, PW * d:PW * (d + half)]).then_inc(S[("ga%d" if on_vector else "gb%d") % k], 1)
+        for k, (ds, n) in enumerate(groups):
+            dst = [(d, T.cores[(first + d) % N]) for d in ds]
+            far = [(d, c) for d, c in dst if c != core]
+            g.wait_ge(S["ga%d" % k], 1)
+            if len(far) == len(dst):
+                g.wait_ge(S["gb%d" % k], 1)
+            use = up if 0 in ds else off
+            send([xfer(c, T.s2[:, PW * d:PW * d + PW], T.land[:, PW * j:PW * j + PW], S["out%d" % (j // 2)], part(use, len(far), i))
+                  for i, (d, c) in enumerate(far)], len(use))
+
+    if rank is not None:
+        def arrivals(m):
+            d = (rank - 2 * chips.index(hubs[m])) % N
+            total = 0
+            for c in mid[m]:
+                if c == core:
+                    continue
+                for ds, n in groups:
+                    if d in ds:
+                        there = len([e for e in ds if T.cores[(2 * chips.index(hubs[m]) + e) % N] != c])
+                        total += len(up if 0 in ds else off) // there
+            return total
+
+        when = lambda m: [1, 2, 3, 0, 4, 5].index((chips.index(chip) - chips.index(hubs[m])) % len(chips))
+        seq = sorted(range(4), key=when)
+        for i, m in enumerate(seq):
+            q, sem = ((g.sync, S.sty), (g.scalar, S.stz))[i % 2]
+            q.wait_ge(S["out%d" % m], arrivals(m))
+            if core in mid[m]:
+                q.wait_ge(S.own1, 1)
+            q.dma_start(T.y[:, 2 * PW * m:2 * PW * (m + 1)], T.land[:, 2 * PW * m:2 * PW * (m + 1)]).then_inc(sem, 16)
+        g.sync.wait_ge(S.sty, 32)
+        g.scalar.wait_ge(S.stz, 32)
+    if sent[0]:
+        g.wait_ge(S.lsem, sent[0])

@@ -4,7 +4,8 @@ from concourse.mybir import AluOpType, ActivationFunctionType
 WORLD = 256
 N = 12
 COLS = 1024
-PW = 128
+PW = 64
+CW = 4 * PW
 ADD = AluOpType.add
 
 SCRATCH = {
@@ -18,23 +19,24 @@ SCRATCH = {
     "a1": ("sbuf", [128, 64], "int32"),
     "b1": ("sbuf", [128, 64], "int32"),
     "l1": ("sbuf", [128, 64], "uint16"),
-    "k2": ("sbuf", [128, 96], "int32"),
-    "c2": ("sbuf", [128, 96], "int32"),
-    "d2": ("sbuf", [128, 96], "int32"),
-    "a2": ("sbuf", [128, 96], "int32"),
-    "m2": ("sbuf", [128, 96], "int32"),
-    "t2": ("sbuf", [128, 96], "int32"),
-    "u2": ("sbuf", [128, 96], "int32"),
-    "w2": ("sbuf", [128, 96], "int32"),
-    "l2": ("sbuf", [128, 96], "uint16"),
+    "k2": ("sbuf", [128, 48], "int32"),
+    "c2": ("sbuf", [128, 48], "int32"),
+    "d2": ("sbuf", [128, 48], "int32"),
+    "a2": ("sbuf", [128, 48], "int32"),
+    "m2": ("sbuf", [128, 48], "int32"),
+    "t2": ("sbuf", [128, 48], "int32"),
+    "u2": ("sbuf", [128, 48], "int32"),
+    "w2": ("sbuf", [128, 48], "int32"),
+    "l2": ("sbuf", [128, 48], "uint16"),
     "xs": ("sbuf", [128, COLS], "float32"),
     "rot": ("sbuf", [128, COLS], "float32"),
-    "rl": ("sbuf", [128, COLS // 2], "float32"),
-    "ex": ("sbuf", [128, PW + N * PW], "float32"),
+    "rl0": ("sbuf", [128, CW], "float32"),
+    "rl1": ("sbuf", [128, CW], "float32"),
+    "ex": ("sbuf", [128, 3 * PW + N * PW], "float32"),
     "s2": ("sbuf", [128, N * PW], "float32"),
     "land": ("sbuf", [128, COLS], "float32"),
 }
-SEMAPHORES = (["hld", "xld", "hb", "io0", "v", "lst1", "lst2", "hand", "harr", "arr", "own0", "own1", "rly", "lsem", "sty", "stz"]
+SEMAPHORES = (["hld", "xld", "hb", "io0", "v", "lst1", "lst2", "hand", "harr", "arr", "own0", "own1", "rly0", "rly1", "lsem", "sty", "stz"]
               + ["tn%d" % k for k in range(4)] + ["ga%d" % k for k in range(4)] + ["gb%d" % k for k in range(4)]
               + ["out%d" % k for k in range(4)])
 
@@ -62,17 +64,32 @@ def layout(T, topo):
     hubs = max((plane(ranks[q][0]) for q in chips), key=len)
     reach = lambda c: all(topo.may_write(c, d) for d in T.cores if d != c)
     on_chip = {q: [c for c in range(WORLD) if where(c) == q] for q in chips}
-    L = {"chips": chips, "ranks": ranks, "hubs": hubs, "where": where, "mid": [], "relay": {}}
+    L = {"chips": chips, "ranks": ranks, "hubs": hubs, "where": where, "mid": [], "relay": {}, "direct": {}, "order": {}}
     for q in hubs:
         a = [c for c in ranks[q] if reach(c)][0]
-        b = [c for c in on_chip[q] if reach(c) and topo.die(c) != topo.die(a) and c not in T.cores][0]
-        L["mid"].append((a, b))
+        b = [c for c in on_chip[q] if reach(c) and topo.die(c) != topo.die(a)][:2]
+        d = [c for c in on_chip[q] if reach(c) and topo.die(c) == topo.die(a) and c not in T.cores][0]
+        L["mid"].append((a, b[0], b[1], d))
     for q in chips:
         if q in hubs:
-            continue
-        for c in ranks[q]:
-            if not reach(c):
-                L["relay"][c] = [d for d in on_chip[q] if reach(d) and topo.die(d) != topo.die(c)][:2]
+            m = hubs.index(q)
+            for i, c in enumerate(ranks[q]):
+                o = [(m + 1 + k) % 4 for k in range(4)]
+                L["relay"][c] = [(L["mid"][m][1 + i], o[0], 0)]
+                L["direct"][c] = o[1:3]
+                L["order"][c] = o
+        else:
+            for c in ranks[q]:
+                o = [0, 1, 2, 3]
+                L["order"][c] = o
+                if reach(c):
+                    d = [e for e in on_chip[q] if reach(e) and topo.die(e) == topo.die(c) and e not in T.cores][0]
+                    L["relay"][c] = [(d, o[0], 0), (d, o[3], 1)]
+                    L["direct"][c] = o[1:3]
+                else:
+                    d = [e for e in on_chip[q] if reach(e) and topo.die(e) != topo.die(c)]
+                    L["relay"][c] = [(d[0], o[0], 0), (d[1], o[1], 0), (d[0], o[2], 1), (d[1], o[3], 1)]
+                    L["direct"][c] = []
     far = [c for c in T.cores if where(c) != chips[0]][0]
     near = on_chip[chips[0]]
     src = [c for c in near if reach(c)][0]
@@ -86,15 +103,14 @@ def rank_program(g, core, T, topo):
     L = layout(T, topo)
     chip = L["where"](core)
     rank = T.rank_of(core)
-    mids = [c for pair in L["mid"] for c in pair]
-    relays = [c for pair in L["relay"].values() for c in pair]
-    if rank is None and core not in mids and core not in relays:
+    mids = [c for four in L["mid"] for c in four]
+    jobs = [(src, m, k) for src in T.cores for d, m, k in L["relay"][src] if d == core]
+    if rank is None and core not in mids and not jobs:
         return
     S = T.sem
     off, up, every = L["off"], L["up"], L["all"]
     hubs, chips, mid = L["hubs"], L["chips"], L["mid"]
-    is_hub = chip in hubs
-    me = hubs.index(chip) if is_hub else None
+    me = hubs.index(chip) if chip in hubs else None
     first = 2 * chips.index(chip)
     sent = [0]
     vn = [0]
@@ -114,7 +130,7 @@ def rank_program(g, core, T, topo):
         vn[0] += 1
 
     def slot(dst_chip, r):
-        a = PW + PW * ((r - 2 * chips.index(dst_chip)) % N)
+        a = 3 * PW + PW * ((r - 2 * chips.index(dst_chip)) % N)
         return T.ex[:, a:a + PW]
 
     def gather(on_vector, out, win, lst):
@@ -122,12 +138,10 @@ def rank_program(g, core, T, topo):
             return g.vector.tensor_copy(out, win.indirect(lst))
         return g.scalar.activation(out, win.indirect(lst), ActivationFunctionType.Copy, bias=-0.0)
 
-    def order(m):
-        return [(m + 1 + k) % 4 for k in range(4)] if m is not None else [0, 1, 2, 3]
-
     if rank is not None:
         g.sync.dma_start(T.hI[0:1, :], T.hh[0:1, :]).then_inc(S.hld, 16)
         g.scalar.dma_start(T.xs[:], T.x[:]).then_inc(S.xld, 16)
+    h_from_first = core in mids and mid[me].index(core) in (1, 2)
     if rank is not None or core in mids:
         n_io = 1
         g.iota(T.pI[:], [[0, 1]], 0, 1).then_inc(S.io0, 1)
@@ -135,12 +149,18 @@ def rank_program(g, core, T, topo):
             g.iota(T.k1[:], [[16, 64]], 0, 0).then_inc(S.io0, 1)
             n_io += 1
         if core in mids:
-            g.iota(T.k2[:], [[1024, 12], [16, 8]], PW * mids.index(core), 0).then_inc(S.io0, 1)
-            g.iota(T.c2[:], [[0, 12], [16, 8]], 0, 0).then_inc(S.io0, 1)
+            g.iota(T.k2[:], [[1024, 12], [16, 4]], PW * mids.index(core), 0).then_inc(S.io0, 1)
+            g.iota(T.c2[:], [[0, 12], [16, 4]], 0, 0).then_inc(S.io0, 1)
             n_io += 2
         if rank is not None:
             g.wait_ge(S.hld, 16)
             g.partition_broadcast(T.hB[:], T.hI[0:1, :], 128).then_inc(S.hb, 1)
+            if me is not None:
+                g.wait_ge(S.hb, 1)
+                if core in mids:
+                    send([xfer(mid[me][3], T.hB[:], T.hB[:], S.harr, part(every, 1, 0))], len(every))
+                else:
+                    send([xfer(mid[me][1 + i], T.hB[:], T.hB[:], S.harr, part(every, 2, i)) for i in (0, 1)], len(every))
         V = g.vector
         V.wait_ge(S.io0, n_io)
         vec(V.tensor_scalar, T.pM[:], T.pI[:], 15, None, AluOpType.bitwise_and)
@@ -150,7 +170,7 @@ def rank_program(g, core, T, topo):
         if rank is not None:
             V.wait_ge(S.hb, 1)
         else:
-            V.wait_ge(S.harr, len(up))
+            V.wait_ge(S.harr, len(every) // (2 if h_from_first else 1))
         vec(V.tensor_copy, T.hF[:], T.hB[:, 0:1])
 
     if rank is not None:
@@ -165,103 +185,107 @@ def rank_program(g, core, T, topo):
         def turn(on_vector, out, a, n):
             return gather(on_vector, out, T.xs[:], T.l1[:, a // 16:(a + n) // 16])
 
-        for k, m in enumerate(order(me)):
-            a = 2 * PW * m
+        o = L["order"][core]
+        for k, m in enumerate(o):
+            a = CW * m
             if m == me and core in mids:
-                turn(k % 2 == 0, T.rot[:, a + PW:a + 2 * PW], a + PW, PW).then_inc(S["tn%d" % k], 1)
+                turn(k % 2 == 0, T.rot[:, a + PW:a + CW], a + PW, CW - PW).then_inc(S["tn%d" % k], 1)
                 turn(k % 2 == 0, slot(chip, rank), a, PW).then_inc(S.own0, 1)
             else:
-                turn(k % 2 == 0, T.rot[:, a:a + 2 * PW], a, 2 * PW).then_inc(S["tn%d" % k], 1)
+                turn(k % 2 == 0, T.rot[:, a:a + CW], a, CW).then_inc(S["tn%d" % k], 1)
 
-    def pieces(buf, a0, ms, r, n):
+    def pieces(buf, a0, ms, r):
         out = []
         for m in ms:
-            for j in (0, 1):
-                a = 2 * PW * m + PW * j - a0
-                out.append(xfer(mid[m][j], buf[:, a:a + PW], slot(hubs[m], r), S.arr, part(off, n, len(out))))
-        return out
+            for j in range(4):
+                a = CW * m + PW * j - a0
+                out.append(xfer(mid[m][j], buf[:, a:a + PW], slot(hubs[m], r), S.arr, part(off, 4 * len(ms), len(out))))
+        send(out, len(off))
+
+    def hand_over(some, engines):
+        for d, m, k in some:
+            g.wait_ge(S["tn%d" % o.index(m)], 1)
+        send([xfer(d, T.rot[:, CW * m:CW * m + CW], T["rl%d" % k][:], S["rly%d" % k], part(engines, len(some), n))
+              for n, (d, m, k) in enumerate(some)], len(engines))
 
     if rank is not None:
-        o = order(me)
-        if core in L["relay"]:
-            for k, d in enumerate(L["relay"][core]):
-                g.wait_ge(S["tn%d" % (2 * k)], 1)
-                g.wait_ge(S["tn%d" % (2 * k + 1)], 1)
-                send([xfer(d, T.rot[:, 512 * k:512 * k + 512], T.rl[:], S.rly, part(every, 1, 0))], len(every))
+        rel, ms = L["relay"][core], L["direct"][core]
+        if not ms:
+            hand_over(rel[0:2], every)
+            hand_over(rel[2:4], every)
         else:
-            g.wait_ge(S.tn0, 1)
-            g.wait_ge(S.tn1, 1)
-            send(pieces(T.rot, 0, o[0:2], rank, 4), len(off))
-            g.wait_ge(S.tn2, 1)
-            if is_hub:
-                send(pieces(T.rot, 0, o[2:3], rank, 2), len(off))
-                g.wait_ge(S.tn3, 1)
-                a = 2 * PW * me
-                if core in mids:
-                    send([xfer(mid[me][1], T.rot[:, a + PW:a + 2 * PW], slot(chip, rank), S.arr, part(up, 1, 0))], len(up))
-                else:
-                    send([xfer(mid[me][1], T.rot[:, a:a + 2 * PW], T.ex[:, 0:2 * PW], S.hand, part(up, 1, 0))], len(up))
-                    g.wait_ge(S.hb, 1)
-                    send([xfer(mid[me][1], T.hB[:], T.hB[:], S.harr, part(up, 1, 0))], len(up))
+            hand_over(rel[0:1], up)
+            for m in ms:
+                g.wait_ge(S["tn%d" % o.index(m)], 1)
+            pieces(T.rot, 0, ms, rank)
+            if rel[1:]:
+                hand_over(rel[1:], up)
+        if me is not None:
+            g.wait_ge(S["tn%d" % o.index(me)], 1)
+            a = CW * me
+            if core in mids:
+                send([xfer(mid[me][j], T.rot[:, a + PW * j:a + PW * j + PW], slot(chip, rank), S.arr, part(up, 4, j)) for j in (1, 2, 3)],
+                     3 * len(up) // 4)
             else:
-                g.wait_ge(S.tn3, 1)
-                send(pieces(T.rot, 0, o[2:4], rank, 4), len(off))
-    for src, pair in L["relay"].items():
-        if core in pair:
-            k = pair.index(core)
-            g.wait_ge(S.rly, len(every))
-            send(pieces(T.rl, 512 * k, [2 * k, 2 * k + 1], T.rank_of(src), 4), len(off))
+                send([xfer(mid[me][3], T.rot[:, a:a + CW], T.ex[:, 0:CW], S.hand, part(up, 1, 0))], len(up))
+    for src, m, k in jobs:
+        g.wait_ge(S["rly%d" % k], len(up))
+        pieces(T["rl%d" % k], CW * m, [m], T.rank_of(src))
 
-    groups = [(range(2, 6), 4), (range(6, 10), 4), (range(10, 12), 2), (range(0, 2), 2)]
+    groups = [range(2, 6), range(6, 10), range(10, 12), range(0, 2)]
     if core in mids:
         j = mids.index(core)
         vec(V.tensor_scalar, T.a2[:], T.k2[:], T.pF[:], T.hF[:], ADD, ADD)
-        vec(V.tensor_scalar, T.m2[:], T.a2[:], 3, 31 * PW, AluOpType.arith_shift_right, AluOpType.bitwise_and)
+        vec(V.tensor_scalar, T.m2[:], T.a2[:], 4, 31 * PW, AluOpType.arith_shift_right, AluOpType.bitwise_and)
         vec(V.tensor_scalar, T.t2[:], T.m2[:], N * PW, -N * PW, AluOpType.is_ge, AluOpType.mult)
         vec(V.tensor_tensor, T.u2[:], T.m2[:], T.t2[:], ADD)
         vec(V.tensor_tensor, T.w2[:], T.u2[:], T.d2[:], ADD)
         V.wait_ge(S.v, vn[0])
         V.tensor_copy(T.l2[:], T.w2[:]).then_inc(S.lst2, 1)
 
+        role = mid[me].index(core)
         expect = 0
         for c in T.cores:
-            w = L["where"](c)
-            if w == chip:
+            if L["where"](c) == chip:
                 continue
-            k = order(hubs.index(w) if w in hubs else None).index(me)
-            expect += len(off) // (2 if (w in hubs and k == 2) else 4)
-        helper = rank is None
-        expect += len(up) if helper else len(off)
-        if helper:
+            if me in L["direct"][c]:
+                expect += len(off) // (4 * len(L["direct"][c]))
+            expect += len([m for d, m, k in L["relay"][c] if m == me]) * (len(off) // 4)
+        if role != 0:
+            expect += len(up) // 4
+        if role != 3:
+            expect += len(off) // 4
+        else:
             other = [c for c in L["ranks"][chip] if c not in mids][0]
             g.wait_ge(S.hand, len(up))
-            send([xfer(mid[me][0], T.ex[:, 0:PW], slot(chip, T.rank_of(other)), S.arr, part(off, 1, 0))], len(off))
+            send([xfer(mid[me][i], T.ex[:, PW * i:PW * i + PW], slot(chip, T.rank_of(other)), S.arr, part(off, 4, i)) for i in (0, 1, 2)],
+                 3 * len(off) // 4)
         for q in (V, g.scalar):
             q.wait_ge(S.lst2, 1)
-            if helper:
+            if role == 3:
                 q.wait_ge(S.hand, len(up))
-            else:
+            if role == 0:
                 q.wait_ge(S.own0, 1)
             q.wait_ge(S.arr, expect)
 
         def pick(on_vector, d, n, out):
-            return gather(on_vector, out, T.ex[:, PW:PW + N * PW], T.l2[:, 8 * d:8 * (d + n)])
+            return gather(on_vector, out, T.ex[:, 3 * PW:3 * PW + N * PW], T.l2[:, 4 * d:4 * (d + n)])
 
-        for k, (ds, n) in enumerate(groups):
+        for k, ds in enumerate(groups):
             half = len(ds) // 2
             for on_vector, d in ((True, ds[0]), (False, ds[half])):
                 if T.cores[(first + d) % N] == core:
                     pick(on_vector, d, half, T.land[:, PW * j:PW * j + PW]).then_inc(S.own1, 1)
                 else:
                     pick(on_vector, d, half, T.s2[:, PW * d:PW * (d + half)]).then_inc(S[("ga%d" if on_vector else "gb%d") % k], 1)
-        for k, (ds, n) in enumerate(groups):
+        for k, ds in enumerate(groups):
             dst = [(d, T.cores[(first + d) % N]) for d in ds]
             far = [(d, c) for d, c in dst if c != core]
             g.wait_ge(S["ga%d" % k], 1)
             if len(far) == len(dst):
                 g.wait_ge(S["gb%d" % k], 1)
             use = up if 0 in ds else off
-            send([xfer(c, T.s2[:, PW * d:PW * d + PW], T.land[:, PW * j:PW * j + PW], S["out%d" % (j // 2)], part(use, len(far), i))
+            send([xfer(c, T.s2[:, PW * d:PW * d + PW], T.land[:, PW * j:PW * j + PW], S["out%d" % (j // 4)], part(use, len(far), i))
                   for i, (d, c) in enumerate(far)], len(use))
 
     if rank is not None:
@@ -271,7 +295,7 @@ def rank_program(g, core, T, topo):
             for c in mid[m]:
                 if c == core:
                     continue
-                for ds, n in groups:
+                for ds in groups:
                     if d in ds:
                         there = len([e for e in ds if T.cores[(2 * chips.index(hubs[m]) + e) % N] != c])
                         total += len(up if 0 in ds else off) // there
@@ -284,7 +308,7 @@ def rank_program(g, core, T, topo):
             q.wait_ge(S["out%d" % m], arrivals(m))
             if core in mid[m]:
                 q.wait_ge(S.own1, 1)
-            q.dma_start(T.y[:, 2 * PW * m:2 * PW * (m + 1)], T.land[:, 2 * PW * m:2 * PW * (m + 1)]).then_inc(sem, 16)
+            q.dma_start(T.y[:, CW * m:CW * (m + 1)], T.land[:, CW * m:CW * (m + 1)]).then_inc(sem, 16)
         g.sync.wait_ge(S.sty, 32)
         g.scalar.wait_ge(S.stz, 32)
     if sent[0]:

@@ -4,8 +4,7 @@ from concourse.mybir import AluOpType, ActivationFunctionType
 WORLD = 256
 N = 12
 COLS = 1024
-PW = 64
-CW = 4 * PW
+WH, WO = 48, 32
 ADD = AluOpType.add
 
 SCRATCH = {
@@ -19,26 +18,27 @@ SCRATCH = {
     "a1": ("sbuf", [128, 64], "int32"),
     "b1": ("sbuf", [128, 64], "int32"),
     "l1": ("sbuf", [128, 64], "uint16"),
-    "k2": ("sbuf", [128, 48], "int32"),
-    "c2": ("sbuf", [128, 48], "int32"),
-    "d2": ("sbuf", [128, 48], "int32"),
-    "a2": ("sbuf", [128, 48], "int32"),
-    "m2": ("sbuf", [128, 48], "int32"),
-    "t2": ("sbuf", [128, 48], "int32"),
-    "u2": ("sbuf", [128, 48], "int32"),
-    "w2": ("sbuf", [128, 48], "int32"),
-    "l2": ("sbuf", [128, 48], "uint16"),
+    "k2": ("sbuf", [128, WH], "int32"),
+    "c2": ("sbuf", [128, WH], "int32"),
+    "d2": ("sbuf", [128, WH], "int32"),
+    "a2": ("sbuf", [128, WH], "int32"),
+    "m2": ("sbuf", [128, WH], "int32"),
+    "t2": ("sbuf", [128, WH], "int32"),
+    "u2": ("sbuf", [128, WH], "int32"),
+    "v2": ("sbuf", [128, WH], "int32"),
+    "w2": ("sbuf", [128, WH], "int32"),
+    "l2": ("sbuf", [128, WH], "uint16"),
     "xs": ("sbuf", [128, COLS], "float32"),
     "rot": ("sbuf", [128, COLS], "float32"),
-    "rl0": ("sbuf", [128, CW], "float32"),
-    "rl1": ("sbuf", [128, CW], "float32"),
-    "ex": ("sbuf", [128, 3 * PW + N * PW], "float32"),
-    "s2": ("sbuf", [128, N * PW], "float32"),
+    "rl0": ("sbuf", [128, 4 * WH], "float32"),
+    "rl1": ("sbuf", [128, 4 * WH], "float32"),
+    "ex": ("sbuf", [128, (3 + N) * WH], "float32"),
+    "s2": ("sbuf", [128, N * WH], "float32"),
     "land": ("sbuf", [128, COLS], "float32"),
 }
 SEMAPHORES = (["hld", "xld", "hb", "io0", "v", "lst1", "lst2", "hand", "harr", "arr", "own0", "own1", "rly0", "rly1", "lsem", "sty", "stz"]
-              + ["tn%d" % k for k in range(4)] + ["ga%d" % k for k in range(4)] + ["gb%d" % k for k in range(4)]
-              + ["out%d" % k for k in range(4)])
+              + ["tn%d" % k for k in range(6)] + ["ga%d" % k for k in range(4)] + ["gb%d" % k for k in range(4)]
+              + ["out%d" % k for k in range(6)])
 
 
 def bits(mask):
@@ -53,65 +53,88 @@ def part(engines, n, i):
     return m
 
 
+def spot(d):
+    return {0: 0, 1: 2, 10: 12, 11: 14}.get(d, d + 2)
+
+
 def layout(T, topo):
     where = lambda c: (topo.host(c), topo.chip(c))
     chips = []
     for c in T.cores:
         if where(c) not in chips:
             chips.append(where(c))
-    ranks = {q: [c for c in T.cores if where(c) == q] for q in chips}
-    plane = lambda a: [q for q in chips if q == where(a) or topo.same_plane(a, ranks[q][0])]
-    hubs = max((plane(ranks[q][0]) for q in chips), key=len)
+    nc = len(chips)
+    ranks = [[c for c in T.cores if where(c) == q] for q in chips]
+    on_chip = [[c for c in range(WORLD) if where(c) == q] for q in chips]
+    plane = lambda a: [i for i in range(nc) if chips[i] == where(a) or topo.same_plane(a, ranks[i][0])]
+    hubs = max((plane(r[0]) for r in ranks), key=len)
+    rest = [i for i in range(nc) if i not in hubs]
     reach = lambda c: all(topo.may_write(c, d) for d in T.cores if d != c)
-    on_chip = {q: [c for c in range(WORLD) if where(c) == q] for q in chips}
-    L = {"chips": chips, "ranks": ranks, "hubs": hubs, "where": where, "mid": [], "relay": {}, "direct": {}, "order": {}}
-    for q in hubs:
-        a = [c for c in ranks[q] if reach(c)][0]
-        b = [c for c in on_chip[q] if reach(c) and topo.die(c) != topo.die(a)][:2]
-        d = [c for c in on_chip[q] if reach(c) and topo.die(c) == topo.die(a) and c not in T.cores][0]
-        L["mid"].append((a, b[0], b[1], d))
-    for q in chips:
-        if q in hubs:
-            m = hubs.index(q)
-            for i, c in enumerate(ranks[q]):
-                o = [(m + 1 + k) % 4 for k in range(4)]
-                L["relay"][c] = [(L["mid"][m][1 + i], o[0], 0)]
-                L["direct"][c] = o[1:3]
-                L["order"][c] = o
-        else:
-            for c in ranks[q]:
-                o = [0, 1, 2, 3]
-                L["order"][c] = o
+    mid = []
+    for i in range(nc):
+        a = [c for c in ranks[i] if reach(c)][0]
+        b = [c for c in on_chip[i] if reach(c) and topo.die(c) != topo.die(a)][:2]
+        d = [c for c in on_chip[i] if reach(c) and topo.die(c) == topo.die(a) and c not in T.cores][0]
+        mid.append((a, b[0], b[1], d))
+    width = [WH if i in hubs else WO for i in range(nc)]
+    start = [0] * nc
+    for k, i in enumerate(hubs):
+        start[i] = 4 * WH * k
+    for k, i in enumerate(rest):
+        start[i] = 4 * WH * len(hubs) + 4 * WO * k
+    calls, order = {}, {}
+    for i in range(nc):
+        far, near, same = mid[i][1], mid[i][2], mid[i][3]
+        free = [e for e in on_chip[i] if topo.die(e) != topo.die(same) and e not in mid[i]]
+        spare = [e for e in on_chip[i] if topo.die(e) == topo.die(same) and e not in mid[i] and e not in T.cores]
+        for c in ranks[i]:
+            if i in hubs:
+                k = hubs.index(i)
+                h = [hubs[(k + 1 + j) % len(hubs)] for j in range(len(hubs) - 1)]
                 if reach(c):
-                    d = [e for e in on_chip[q] if reach(e) and topo.die(e) == topo.die(c) and e not in T.cores][0]
-                    L["relay"][c] = [(d, o[0], 0), (d, o[3], 1)]
-                    L["direct"][c] = o[1:3]
+                    calls[c] = [("hand", [(free[1], h[0], 0)]), ("hand", [(near, rest[1], 0)]), ("direct", h[1:3]), ("direct", rest[0:1])]
+                    order[c] = [h[0], rest[1], h[1], h[2], rest[0], i]
                 else:
-                    d = [e for e in on_chip[q] if reach(e) and topo.die(e) != topo.die(c)]
-                    L["relay"][c] = [(d[0], o[0], 0), (d[1], o[1], 0), (d[0], o[2], 1), (d[1], o[3], 1)]
-                    L["direct"][c] = []
-    far = [c for c in T.cores if where(c) != chips[0]][0]
-    near = on_chip[chips[0]]
-    src = [c for c in near if reach(c)][0]
-    L["off"] = bits(topo.mask(src, far))
-    L["all"] = bits(topo.mask(src, [c for c in near if c != src][0]))
-    L["up"] = [e for e in L["all"] if e not in L["off"]]
-    return L
+                    calls[c] = [("hand", [(free[0], h[0], 0)]), ("hand", [(same, rest[0], 0), (far, rest[1], 0)]), ("direct", h[1:3])]
+                    order[c] = [h[0]] + rest + h[1:3] + [i]
+            else:
+                k = 2 * rest.index(i) + (1 if reach(c) else 0)
+                h = [hubs[(k + j) % len(hubs)] for j in range(len(hubs))]
+                others = [j for j in rest if j != i]
+                if reach(c):
+                    calls[c] = [("hand", [(same, h[0], 0)]), ("hand", [(spare[0], others[0], 0)]), ("direct", h[1:3]), ("direct", h[3:4])]
+                    order[c] = [h[0], others[0]] + h[1:] + [i]
+                else:
+                    calls[c] = [("hand", [(far, h[0], 0), (near, h[1], 0)]), ("hand", [(far, h[2], 1), (near, h[3], 1)]), ("direct", others)]
+                    order[c] = h + others + [i]
+    a, b = mid[0][0], mid[0][1]
+    off, every = bits(topo.mask(a, mid[1][0])), bits(topo.mask(a, b))
+    return {"chips": chips, "ranks": ranks, "where": where, "mid": mid, "width": width, "start": start, "calls": calls, "order": order,
+            "off": off,
+            "all": every, "up": [e for e in every if e not in off]}
 
 
 def rank_program(g, core, T, topo):
     L = layout(T, topo)
-    chip = L["where"](core)
+    if L["where"](core) not in L["chips"]:
+        return
+    me = L["chips"].index(L["where"](core))
     rank = T.rank_of(core)
-    mids = [c for four in L["mid"] for c in four]
-    jobs = [(src, m, k) for src in T.cores for d, m, k in L["relay"][src] if d == core]
-    if rank is None and core not in mids and not jobs:
+    off, up, every = L["off"], L["up"], L["all"]
+    mid, width, start = L["mid"], L["width"], L["start"]
+    in_mid = core in mid[me]
+
+    def hand_engines(c):
+        return up if [1 for kind, arg in L["calls"][c] if kind == "direct" and len(arg) > 1] else every
+
+    jobs = []
+    for src in T.cores:
+        for kind, arg in L["calls"][src]:
+            if kind == "hand":
+                jobs += [(src, m, k, len(hand_engines(src)) // len(arg)) for d, m, k in arg if d == core]
+    if rank is None and not in_mid and not jobs:
         return
     S = T.sem
-    off, up, every = L["off"], L["up"], L["all"]
-    hubs, chips, mid = L["hubs"], L["chips"], L["mid"]
-    me = hubs.index(chip) if chip in hubs else None
-    first = 2 * chips.index(chip)
     sent = [0]
     vn = [0]
 
@@ -129,48 +152,49 @@ def rank_program(g, core, T, topo):
         call(*args).then_inc(S.v, 1)
         vn[0] += 1
 
-    def slot(dst_chip, r):
-        a = 3 * PW + PW * ((r - 2 * chips.index(dst_chip)) % N)
-        return T.ex[:, a:a + PW]
+    def slot(m, r):
+        a = width[m] * (3 + (r - 2 * m) % N)
+        return T.ex[:, a:a + width[m]]
 
     def gather(on_vector, out, win, lst):
         if on_vector:
             return g.vector.tensor_copy(out, win.indirect(lst))
         return g.scalar.activation(out, win.indirect(lst), ActivationFunctionType.Copy, bias=-0.0)
 
+    w = width[me]
+    wc = w // 16
     if rank is not None:
         g.sync.dma_start(T.hI[0:1, :], T.hh[0:1, :]).then_inc(S.hld, 16)
         g.scalar.dma_start(T.xs[:], T.x[:]).then_inc(S.xld, 16)
-    h_from_first = core in mids and mid[me].index(core) in (1, 2)
-    if rank is not None or core in mids:
+    if rank is not None or in_mid:
         n_io = 1
         g.iota(T.pI[:], [[0, 1]], 0, 1).then_inc(S.io0, 1)
         if rank is not None:
             g.iota(T.k1[:], [[16, 64]], 0, 0).then_inc(S.io0, 1)
             n_io += 1
-        if core in mids:
-            g.iota(T.k2[:], [[1024, 12], [16, 4]], PW * mids.index(core), 0).then_inc(S.io0, 1)
-            g.iota(T.c2[:], [[0, 12], [16, 4]], 0, 0).then_inc(S.io0, 1)
-            n_io += 2
+        if in_mid:
+            p0 = start[me] + w * mid[me].index(core)
+            g.iota(T.k2[:, 0:4 * wc], [[COLS, 2], [0, 2], [16, wc]], p0, 0).then_inc(S.io0, 1)
+            g.iota(T.k2[:, 4 * wc:12 * wc], [[COLS, 8], [16, wc]], p0 + 2 * COLS, 0).then_inc(S.io0, 1)
+            g.iota(T.k2[:, 12 * wc:16 * wc], [[COLS, 2], [0, 2], [16, wc]], p0 + 10 * COLS, 0).then_inc(S.io0, 1)
+            g.iota(T.c2[:, 0:16 * wc], [[0, 16], [16, wc]], 0, 0).then_inc(S.io0, 1)
+            n_io += 4
         if rank is not None:
             g.wait_ge(S.hld, 16)
             g.partition_broadcast(T.hB[:], T.hI[0:1, :], 128).then_inc(S.hb, 1)
-            if me is not None:
-                g.wait_ge(S.hb, 1)
-                if core in mids:
-                    send([xfer(mid[me][3], T.hB[:], T.hB[:], S.harr, part(every, 1, 0))], len(every))
-                else:
-                    send([xfer(mid[me][1 + i], T.hB[:], T.hB[:], S.harr, part(every, 2, i)) for i in (0, 1)], len(every))
+            g.wait_ge(S.hb, 1)
+            to = mid[me][3:] if in_mid else mid[me][1:3]
+            send([xfer(d, T.hB[:], T.hB[:], S.harr, part(every, len(to), i)) for i, d in enumerate(to)], len(every))
         V = g.vector
         V.wait_ge(S.io0, n_io)
         vec(V.tensor_scalar, T.pM[:], T.pI[:], 15, None, AluOpType.bitwise_and)
         vec(V.tensor_copy, T.pF[:], T.pM[:])
-        if core in mids:
-            vec(V.tensor_scalar, T.d2[:], T.c2[:], T.pF[:], None, ADD)
+        if in_mid:
+            vec(V.tensor_scalar, T.d2[:, 0:16 * wc], T.c2[:, 0:16 * wc], T.pF[:], None, ADD)
         if rank is not None:
             V.wait_ge(S.hb, 1)
         else:
-            V.wait_ge(S.harr, len(every) // (2 if h_from_first else 1))
+            V.wait_ge(S.harr, len(every) // (1 if core == mid[me][3] else 2))
         vec(V.tensor_copy, T.hF[:], T.hB[:, 0:1])
 
     if rank is not None:
@@ -187,78 +211,68 @@ def rank_program(g, core, T, topo):
 
         o = L["order"][core]
         for k, m in enumerate(o):
-            a = CW * m
-            if m == me and core in mids:
-                turn(k % 2 == 0, T.rot[:, a + PW:a + CW], a + PW, CW - PW).then_inc(S["tn%d" % k], 1)
-                turn(k % 2 == 0, slot(chip, rank), a, PW).then_inc(S.own0, 1)
-            else:
-                turn(k % 2 == 0, T.rot[:, a:a + CW], a, CW).then_inc(S["tn%d" % k], 1)
+            a, n = start[m], 4 * width[m]
+            turn(k % 2 == 0, T.rot[:, a:a + n], a, n).then_inc(S["tn%d" % k], 1)
+            if m == me and in_mid:
+                turn(k % 2 == 0, slot(me, rank), a, w).then_inc(S.own0, 1)
 
     def pieces(buf, a0, ms, r):
         out = []
         for m in ms:
             for j in range(4):
-                a = CW * m + PW * j - a0
-                out.append(xfer(mid[m][j], buf[:, a:a + PW], slot(hubs[m], r), S.arr, part(off, 4 * len(ms), len(out))))
+                a = start[m] + width[m] * j - a0
+                out.append(xfer(mid[m][j], buf[:, a:a + width[m]], slot(m, r), S.arr, part(off, 4 * len(ms), len(out))))
         send(out, len(off))
 
-    def hand_over(some, engines):
-        for d, m, k in some:
-            g.wait_ge(S["tn%d" % o.index(m)], 1)
-        send([xfer(d, T.rot[:, CW * m:CW * m + CW], T["rl%d" % k][:], S["rly%d" % k], part(engines, len(some), n))
-              for n, (d, m, k) in enumerate(some)], len(engines))
-
     if rank is not None:
-        rel, ms = L["relay"][core], L["direct"][core]
-        if not ms:
-            hand_over(rel[0:2], every)
-            hand_over(rel[2:4], every)
-        else:
-            hand_over(rel[0:1], up)
-            for m in ms:
+        for kind, arg in L["calls"][core]:
+            for m in arg if kind == "direct" else [b for a, b, c in arg]:
                 g.wait_ge(S["tn%d" % o.index(m)], 1)
-            pieces(T.rot, 0, ms, rank)
-            if rel[1:]:
-                hand_over(rel[1:], up)
-        if me is not None:
-            g.wait_ge(S["tn%d" % o.index(me)], 1)
-            a = CW * me
-            if core in mids:
-                send([xfer(mid[me][j], T.rot[:, a + PW * j:a + PW * j + PW], slot(chip, rank), S.arr, part(up, 4, j)) for j in (1, 2, 3)],
-                     3 * len(up) // 4)
+            if kind == "direct":
+                pieces(T.rot, 0, arg, rank)
             else:
-                send([xfer(mid[me][3], T.rot[:, a:a + CW], T.ex[:, 0:CW], S.hand, part(up, 1, 0))], len(up))
-    for src, m, k in jobs:
-        g.wait_ge(S["rly%d" % k], len(up))
-        pieces(T["rl%d" % k], CW * m, [m], T.rank_of(src))
+                eng = hand_engines(core)
+                send([xfer(d, T.rot[:, start[m]:start[m] + 4 * width[m]], T["rl%d" % k][:, 0:4 * width[m]], S["rly%d" % k],
+                           part(eng, len(arg), n)) for n, (d, m, k) in enumerate(arg)], len(eng))
+        g.wait_ge(S["tn%d" % o.index(me)], 1)
+        a = start[me]
+        if in_mid:
+            send([xfer(mid[me][j], T.rot[:, a + w * j:a + w * j + w], slot(me, rank), S.arr, part(up, 4, j)) for j in (1, 2, 3)],
+                 3 * len(up) // 4)
+        else:
+            send([xfer(mid[me][3], T.rot[:, a:a + 4 * w], T.ex[:, 0:4 * w], S.hand, part(up, 1, 0))], len(up))
+    for src, m, k, n in jobs:
+        g.wait_ge(S["rly%d" % k], n)
+        pieces(T["rl%d" % k], start[m], [m], T.rank_of(src))
 
     groups = [range(2, 6), range(6, 10), range(10, 12), range(0, 2)]
-    if core in mids:
-        j = mids.index(core)
-        vec(V.tensor_scalar, T.a2[:], T.k2[:], T.pF[:], T.hF[:], ADD, ADD)
-        vec(V.tensor_scalar, T.m2[:], T.a2[:], 4, 31 * PW, AluOpType.arith_shift_right, AluOpType.bitwise_and)
-        vec(V.tensor_scalar, T.t2[:], T.m2[:], N * PW, -N * PW, AluOpType.is_ge, AluOpType.mult)
-        vec(V.tensor_tensor, T.u2[:], T.m2[:], T.t2[:], ADD)
-        vec(V.tensor_tensor, T.w2[:], T.u2[:], T.d2[:], ADD)
+    if in_mid:
+        z = slice(0, 16 * wc)
+        vec(V.tensor_scalar, T.a2[:, z], T.k2[:, z], T.pF[:], T.hF[:], ADD, ADD)
+        vec(V.tensor_scalar, T.m2[:, z], T.a2[:, z], 10, None, AluOpType.arith_shift_right)
+        vec(V.tensor_scalar, T.t2[:, z], T.m2[:, z], N, -N, AluOpType.is_ge, AluOpType.mult)
+        vec(V.tensor_tensor, T.u2[:, z], T.m2[:, z], T.t2[:, z], ADD)
+        vec(V.tensor_scalar, T.v2[:, z], T.u2[:, z], w, None, AluOpType.mult)
+        vec(V.tensor_tensor, T.w2[:, z], T.v2[:, z], T.d2[:, z], ADD)
         V.wait_ge(S.v, vn[0])
-        V.tensor_copy(T.l2[:], T.w2[:]).then_inc(S.lst2, 1)
+        V.tensor_copy(T.l2[:, z], T.w2[:, z]).then_inc(S.lst2, 1)
 
         role = mid[me].index(core)
         expect = 0
         for c in T.cores:
-            if L["where"](c) == chip:
-                continue
-            if me in L["direct"][c]:
-                expect += len(off) // (4 * len(L["direct"][c]))
-            expect += len([m for d, m, k in L["relay"][c] if m == me]) * (len(off) // 4)
+            for kind, arg in L["calls"][c]:
+                if kind == "direct" and me in arg:
+                    expect += len(off) // (4 * len(arg))
+                if kind == "hand":
+                    expect += len([m for d, m, k in arg if m == me]) * (len(off) // 4)
         if role != 0:
             expect += len(up) // 4
         if role != 3:
             expect += len(off) // 4
         else:
-            other = [c for c in L["ranks"][chip] if c not in mids][0]
+            other = [c for c in L["ranks"][me] if c not in mid[me]][0]
             g.wait_ge(S.hand, len(up))
-            send([xfer(mid[me][i], T.ex[:, PW * i:PW * i + PW], slot(chip, T.rank_of(other)), S.arr, part(off, 4, i)) for i in (0, 1, 2)],
+            send([xfer(mid[me][i], T.ex[:, w * i:w * i + w], slot(me, T.rank_of(other)), S.arr, part(off, 4, i)) for i in (0, 1, 2)],
                  3 * len(off) // 4)
         for q in (V, g.scalar):
             q.wait_ge(S.lst2, 1)
@@ -269,47 +283,46 @@ def rank_program(g, core, T, topo):
             q.wait_ge(S.arr, expect)
 
         def pick(on_vector, d, n, out):
-            return gather(on_vector, out, T.ex[:, 3 * PW:3 * PW + N * PW], T.l2[:, 4 * d:4 * (d + n)])
+            return gather(on_vector, out, T.ex[:, 3 * w:(3 + N) * w], T.l2[:, wc * spot(d):wc * (spot(d) + n)])
 
+        mine = start[me] + w * role
         for k, ds in enumerate(groups):
             half = len(ds) // 2
             for on_vector, d in ((True, ds[0]), (False, ds[half])):
-                if T.cores[(first + d) % N] == core:
-                    pick(on_vector, d, half, T.land[:, PW * j:PW * j + PW]).then_inc(S.own1, 1)
+                if T.cores[(2 * me + d) % N] == core:
+                    pick(on_vector, d, half, T.land[:, mine:mine + w]).then_inc(S.own1, 1)
                 else:
-                    pick(on_vector, d, half, T.s2[:, PW * d:PW * (d + half)]).then_inc(S[("ga%d" if on_vector else "gb%d") % k], 1)
+                    pick(on_vector, d, half, T.s2[:, w * d:w * (d + half)]).then_inc(S[("ga%d" if on_vector else "gb%d") % k], 1)
         for k, ds in enumerate(groups):
-            dst = [(d, T.cores[(first + d) % N]) for d in ds]
+            dst = [(d, T.cores[(2 * me + d) % N]) for d in ds]
             far = [(d, c) for d, c in dst if c != core]
             g.wait_ge(S["ga%d" % k], 1)
             if len(far) == len(dst):
                 g.wait_ge(S["gb%d" % k], 1)
             use = up if 0 in ds else off
-            send([xfer(c, T.s2[:, PW * d:PW * d + PW], T.land[:, PW * j:PW * j + PW], S["out%d" % (j // 4)], part(use, len(far), i))
+            send([xfer(c, T.s2[:, w * d:w * d + w], T.land[:, mine:mine + w], S["out%d" % me], part(use, len(far), i))
                   for i, (d, c) in enumerate(far)], len(use))
 
     if rank is not None:
         def arrivals(m):
-            d = (rank - 2 * chips.index(hubs[m])) % N
+            d = (rank - 2 * m) % N
             total = 0
             for c in mid[m]:
-                if c == core:
-                    continue
                 for ds in groups:
-                    if d in ds:
-                        there = len([e for e in ds if T.cores[(2 * chips.index(hubs[m]) + e) % N] != c])
-                        total += len(up if 0 in ds else off) // there
+                    if c != core and d in ds:
+                        total += len(up if 0 in ds else off) // len([e for e in ds if T.cores[(2 * m + e) % N] != c])
             return total
 
-        when = lambda m: [1, 2, 3, 0, 4, 5].index((chips.index(chip) - chips.index(hubs[m])) % len(chips))
-        seq = sorted(range(4), key=when)
+        nc = len(mid)
+        seq = sorted(range(nc), key=lambda m: [1, 2, 3, 0, 4, 5].index((me - m) % nc))
         for i, m in enumerate(seq):
             q, sem = ((g.sync, S.sty), (g.scalar, S.stz))[i % 2]
             q.wait_ge(S["out%d" % m], arrivals(m))
             if core in mid[m]:
                 q.wait_ge(S.own1, 1)
-            q.dma_start(T.y[:, CW * m:CW * (m + 1)], T.land[:, CW * m:CW * (m + 1)]).then_inc(sem, 16)
-        g.sync.wait_ge(S.sty, 32)
-        g.scalar.wait_ge(S.stz, 32)
+            a, n = start[m], 4 * width[m]
+            q.dma_start(T.y[:, a:a + n], T.land[:, a:a + n]).then_inc(sem, 16)
+        g.sync.wait_ge(S.sty, 16 * (nc // 2))
+        g.scalar.wait_ge(S.stz, 16 * (nc // 2))
     if sent[0]:
         g.wait_ge(S.lsem, sent[0])

from concourse.bass import DstId, RemoteDMATransfer
from concourse.mybir import AluOpType, ActivationFunctionType

WORLD = 256
N = 12
COLS = 1024
WH, WO = 48, 32
ADD = AluOpType.add

SCRATCH = {
    "hI": ("sbuf", [16, 2], "int32"),
    "hB": ("sbuf", [128, 2], "int32"),
    "hF": ("sbuf", [128, 1], "float32"),
    "pI": ("sbuf", [128, 1], "int32"),
    "pM": ("sbuf", [128, 1], "int32"),
    "pF": ("sbuf", [128, 1], "float32"),
    "k1": ("sbuf", [128, 64], "int32"),
    "a1": ("sbuf", [128, 64], "int32"),
    "b1": ("sbuf", [128, 64], "int32"),
    "l1": ("sbuf", [128, 64], "uint16"),
    "k2": ("sbuf", [128, WH], "int32"),
    "c2": ("sbuf", [128, WH], "int32"),
    "d2": ("sbuf", [128, WH], "int32"),
    "a2": ("sbuf", [128, WH], "int32"),
    "m2": ("sbuf", [128, WH], "int32"),
    "t2": ("sbuf", [128, WH], "int32"),
    "u2": ("sbuf", [128, WH], "int32"),
    "v2": ("sbuf", [128, WH], "int32"),
    "w2": ("sbuf", [128, WH], "int32"),
    "l2": ("sbuf", [128, WH], "uint16"),
    "xs": ("sbuf", [128, COLS], "float32"),
    "rot": ("sbuf", [128, COLS], "float32"),
    "rl0": ("sbuf", [128, 4 * WH], "float32"),
    "rl1": ("sbuf", [128, 4 * WH], "float32"),
    "ex": ("sbuf", [128, (3 + N) * WH], "float32"),
    "s2": ("sbuf", [128, N * WH], "float32"),
    "land": ("sbuf", [128, COLS], "float32"),
}
SEMAPHORES = (["hld", "xld", "hb", "io0", "v", "lst1", "lst2", "hand", "harr", "arr", "own0", "own1", "rly0", "rly1", "lsem", "sty", "stz"]
              + ["tn%d" % k for k in range(6)] + ["ga%d" % k for k in range(4)] + ["gb%d" % k for k in range(4)]
              + ["out%d" % k for k in range(6)])


def bits(mask):
    return [e for e in range(16) if (mask >> e) & 1]


def part(engines, n, i):
    w = len(engines) // n
    m = 0
    for e in engines[i * w:(i + 1) * w]:
        m |= 1 << e
    return m


def spot(d):
    return {0: 0, 1: 2, 10: 12, 11: 14}.get(d, d + 2)


def layout(T, topo):
    where = lambda c: (topo.host(c), topo.chip(c))
    chips = []
    for c in T.cores:
        if where(c) not in chips:
            chips.append(where(c))
    nc = len(chips)
    ranks = [[c for c in T.cores if where(c) == q] for q in chips]
    on_chip = [[c for c in range(WORLD) if where(c) == q] for q in chips]
    plane = lambda a: [i for i in range(nc) if chips[i] == where(a) or topo.same_plane(a, ranks[i][0])]
    hubs = max((plane(r[0]) for r in ranks), key=len)
    rest = [i for i in range(nc) if i not in hubs]
    reach = lambda c: all(topo.may_write(c, d) for d in T.cores if d != c)
    mid = []
    for i in range(nc):
        a = [c for c in ranks[i] if reach(c)][0]
        b = [c for c in on_chip[i] if reach(c) and topo.die(c) != topo.die(a)][:2]
        d = [c for c in on_chip[i] if reach(c) and topo.die(c) == topo.die(a) and c not in T.cores][0]
        mid.append((a, b[0], b[1], d))
    width = [WH if i in hubs else WO for i in range(nc)]
    start = [0] * nc
    for k, i in enumerate(hubs):
        start[i] = 4 * WH * k
    for k, i in enumerate(rest):
        start[i] = 4 * WH * len(hubs) + 4 * WO * k
    calls, order = {}, {}
    for i in range(nc):
        far, near, same = mid[i][1], mid[i][2], mid[i][3]
        free = [e for e in on_chip[i] if topo.die(e) != topo.die(same) and e not in mid[i]]
        spare = [e for e in on_chip[i] if topo.die(e) == topo.die(same) and e not in mid[i] and e not in T.cores]
        for c in ranks[i]:
            if i in hubs:
                k = hubs.index(i)
                h = [hubs[(k + 1 + j) % len(hubs)] for j in range(len(hubs) - 1)]
                if reach(c):
                    calls[c] = [("hand", [(free[1], h[0], 0)]), ("hand", [(near, rest[1], 0)]), ("direct", h[1:3]), ("direct", rest[0:1])]
                    order[c] = [h[0], rest[1], h[1], h[2], rest[0], i]
                else:
                    calls[c] = [("hand", [(free[0], h[0], 0)]), ("hand", [(same, rest[0], 0), (far, rest[1], 0)]), ("direct", h[1:3])]
                    order[c] = [h[0]] + rest + h[1:3] + [i]
            else:
                k = 2 * rest.index(i) + (1 if reach(c) else 0)
                h = [hubs[(k + j) % len(hubs)] for j in range(len(hubs))]
                others = [j for j in rest if j != i]
                if reach(c):
                    calls[c] = [("hand", [(same, h[0], 0)]), ("hand", [(spare[0], others[0], 0)]), ("direct", h[1:3]), ("direct", h[3:4])]
                    order[c] = [h[0], others[0]] + h[1:] + [i]
                else:
                    calls[c] = [("hand", [(far, h[0], 0), (near, h[1], 0)]), ("hand", [(far, h[2], 1), (near, h[3], 1)]), ("direct", others)]
                    order[c] = h + others + [i]
    a, b = mid[0][0], mid[0][1]
    off, every = bits(topo.mask(a, mid[1][0])), bits(topo.mask(a, b))
    return {"chips": chips, "ranks": ranks, "where": where, "mid": mid, "width": width, "start": start, "calls": calls, "order": order,
            "off": off,
            "all": every, "up": [e for e in every if e not in off]}


def rank_program(g, core, T, topo):
    L = layout(T, topo)
    if L["where"](core) not in L["chips"]:
        return
    me = L["chips"].index(L["where"](core))
    rank = T.rank_of(core)
    off, up, every = L["off"], L["up"], L["all"]
    mid, width, start = L["mid"], L["width"], L["start"]
    in_mid = core in mid[me]

    def hand_engines(c):
        return up if [1 for kind, arg in L["calls"][c] if kind == "direct" and len(arg) > 1] else every

    jobs = []
    for src in T.cores:
        for kind, arg in L["calls"][src]:
            if kind == "hand":
                jobs += [(src, m, k, len(hand_engines(src)) // len(arg)) for d, m, k in arg if d == core]
    if rank is None and not in_mid and not jobs:
        return
    S = T.sem
    sent = [0]
    vn = [0]

    def xfer(dst, src_ap, dst_ap, sem, mask):
        rid, pid = topo.addr(dst, core)
        return RemoteDMATransfer(dst_ids=[DstId(rid=rid, pnc=pid)], dma_engine_mask=mask, remote_sem=sem, src=src_ap, dst=dst_ap)

    def send(transfers, engines):
        g.remote_dma_fused(transfers, local_sem=S.lsem)
        sent[0] += engines

    def vec(call, *args):
        if vn[0]:
            g.vector.wait_ge(S.v, vn[0])
        call(*args).then_inc(S.v, 1)
        vn[0] += 1

    def slot(m, r):
        a = width[m] * (3 + (r - 2 * m) % N)
        return T.ex[:, a:a + width[m]]

    def gather(on_vector, out, win, lst):
        if on_vector:
            return g.vector.tensor_copy(out, win.indirect(lst))
        return g.scalar.activation(out, win.indirect(lst), ActivationFunctionType.Copy, bias=-0.0)

    w = width[me]
    wc = w // 16
    if rank is not None:
        g.sync.dma_start(T.hI[0:1, :], T.hh[0:1, :]).then_inc(S.hld, 16)
        g.scalar.dma_start(T.xs[:], T.x[:]).then_inc(S.xld, 16)
    if rank is not None or in_mid:
        n_io = 1
        g.iota(T.pI[:], [[0, 1]], 0, 1).then_inc(S.io0, 1)
        if rank is not None:
            g.iota(T.k1[:], [[16, 64]], 0, 0).then_inc(S.io0, 1)
            n_io += 1
        if in_mid:
            p0 = start[me] + w * mid[me].index(core)
            g.iota(T.k2[:, 0:4 * wc], [[COLS, 2], [0, 2], [16, wc]], p0, 0).then_inc(S.io0, 1)
            g.iota(T.k2[:, 4 * wc:12 * wc], [[COLS, 8], [16, wc]], p0 + 2 * COLS, 0).then_inc(S.io0, 1)
            g.iota(T.k2[:, 12 * wc:16 * wc], [[COLS, 2], [0, 2], [16, wc]], p0 + 10 * COLS, 0).then_inc(S.io0, 1)
            g.iota(T.c2[:, 0:16 * wc], [[0, 16], [16, wc]], 0, 0).then_inc(S.io0, 1)
            n_io += 4
        if rank is not None:
            g.wait_ge(S.hld, 16)
            g.partition_broadcast(T.hB[:], T.hI[0:1, :], 128).then_inc(S.hb, 1)
            g.wait_ge(S.hb, 1)
            to = mid[me][3:] if in_mid else mid[me][1:3]
            send([xfer(d, T.hB[:], T.hB[:], S.harr, part(every, len(to), i)) for i, d in enumerate(to)], len(every))
        V = g.vector
        V.wait_ge(S.io0, n_io)
        vec(V.tensor_scalar, T.pM[:], T.pI[:], 15, None, AluOpType.bitwise_and)
        vec(V.tensor_copy, T.pF[:], T.pM[:])
        if in_mid:
            vec(V.tensor_scalar, T.d2[:, 0:16 * wc], T.c2[:, 0:16 * wc], T.pF[:], None, ADD)
        if rank is not None:
            V.wait_ge(S.hb, 1)
        else:
            V.wait_ge(S.harr, len(every) // (1 if core == mid[me][3] else 2))
        vec(V.tensor_copy, T.hF[:], T.hB[:, 0:1])

    if rank is not None:
        vec(V.tensor_scalar, T.a1[:], T.k1[:], T.pF[:], T.hF[:], ADD, ADD)
        vec(V.tensor_scalar, T.b1[:], T.a1[:], COLS - 1, None, AluOpType.bitwise_and)
        V.wait_ge(S.v, vn[0])
        V.tensor_copy(T.l1[:], T.b1[:]).then_inc(S.lst1, 1)
        for q in (V, g.scalar):
            q.wait_ge(S.lst1, 1)
            q.wait_ge(S.xld, 16)

        def turn(on_vector, out, a, n):
            return gather(on_vector, out, T.xs[:], T.l1[:, a // 16:(a + n) // 16])

        o = L["order"][core]
        for k, m in enumerate(o):
            a, n = start[m], 4 * width[m]
            turn(k % 2 == 0, T.rot[:, a:a + n], a, n).then_inc(S["tn%d" % k], 1)
            if m == me and in_mid:
                turn(k % 2 == 0, slot(me, rank), a, w).then_inc(S.own0, 1)

    def pieces(buf, a0, ms, r):
        out = []
        for m in ms:
            for j in range(4):
                a = start[m] + width[m] * j - a0
                out.append(xfer(mid[m][j], buf[:, a:a + width[m]], slot(m, r), S.arr, part(off, 4 * len(ms), len(out))))
        send(out, len(off))

    if rank is not None:
        for kind, arg in L["calls"][core]:
            for m in arg if kind == "direct" else [b for a, b, c in arg]:
                g.wait_ge(S["tn%d" % o.index(m)], 1)
            if kind == "direct":
                pieces(T.rot, 0, arg, rank)
            else:
                eng = hand_engines(core)
                send([xfer(d, T.rot[:, start[m]:start[m] + 4 * width[m]], T["rl%d" % k][:, 0:4 * width[m]], S["rly%d" % k],
                           part(eng, len(arg), n)) for n, (d, m, k) in enumerate(arg)], len(eng))
        g.wait_ge(S["tn%d" % o.index(me)], 1)
        a = start[me]
        if in_mid:
            send([xfer(mid[me][j], T.rot[:, a + w * j:a + w * j + w], slot(me, rank), S.arr, part(up, 4, j)) for j in (1, 2, 3)],
                 3 * len(up) // 4)
        else:
            send([xfer(mid[me][3], T.rot[:, a:a + 4 * w], T.ex[:, 0:4 * w], S.hand, part(up, 1, 0))], len(up))
    for src, m, k, n in jobs:
        g.wait_ge(S["rly%d" % k], n)
        pieces(T["rl%d" % k], start[m], [m], T.rank_of(src))

    groups = [range(2, 6), range(6, 10), range(10, 12), range(0, 2)]
    if in_mid:
        z = slice(0, 16 * wc)
        vec(V.tensor_scalar, T.a2[:, z], T.k2[:, z], T.pF[:], T.hF[:], ADD, ADD)
        vec(V.tensor_scalar, T.m2[:, z], T.a2[:, z], 10, None, AluOpType.arith_shift_right)
        vec(V.tensor_scalar, T.t2[:, z], T.m2[:, z], N, -N, AluOpType.is_ge, AluOpType.mult)
        vec(V.tensor_tensor, T.u2[:, z], T.m2[:, z], T.t2[:, z], ADD)
        vec(V.tensor_scalar, T.v2[:, z], T.u2[:, z], w, None, AluOpType.mult)
        vec(V.tensor_tensor, T.w2[:, z], T.v2[:, z], T.d2[:, z], ADD)
        V.wait_ge(S.v, vn[0])
        V.tensor_copy(T.l2[:, z], T.w2[:, z]).then_inc(S.lst2, 1)

        role = mid[me].index(core)
        expect = 0
        for c in T.cores:
            for kind, arg in L["calls"][c]:
                if kind == "direct" and me in arg:
                    expect += len(off) // (4 * len(arg))
                if kind == "hand":
                    expect += len([m for d, m, k in arg if m == me]) * (len(off) // 4)
        if role != 0:
            expect += len(up) // 4
        if role != 3:
            expect += len(off) // 4
        else:
            other = [c for c in L["ranks"][me] if c not in mid[me]][0]
            g.wait_ge(S.hand, len(up))
            send([xfer(mid[me][i], T.ex[:, w * i:w * i + w], slot(me, T.rank_of(other)), S.arr, part(off, 4, i)) for i in (0, 1, 2)],
                 3 * len(off) // 4)
        for q in (V, g.scalar):
            q.wait_ge(S.lst2, 1)
            if role == 3:
                q.wait_ge(S.hand, len(up))
            if role == 0:
                q.wait_ge(S.own0, 1)
            q.wait_ge(S.arr, expect)

        def pick(on_vector, d, n, out):
            return gather(on_vector, out, T.ex[:, 3 * w:(3 + N) * w], T.l2[:, wc * spot(d):wc * (spot(d) + n)])

        mine = start[me] + w * role
        for k, ds in enumerate(groups):
            half = len(ds) // 2
            for on_vector, d in ((True, ds[0]), (False, ds[half])):
                if T.cores[(2 * me + d) % N] == core:
                    pick(on_vector, d, half, T.land[:, mine:mine + w]).then_inc(S.own1, 1)
                else:
                    pick(on_vector, d, half, T.s2[:, w * d:w * (d + half)]).then_inc(S[("ga%d" if on_vector else "gb%d") % k], 1)
        for k, ds in enumerate(groups):
            dst = [(d, T.cores[(2 * me + d) % N]) for d in ds]
            far = [(d, c) for d, c in dst if c != core]
            g.wait_ge(S["ga%d" % k], 1)
            if len(far) == len(dst):
                g.wait_ge(S["gb%d" % k], 1)
            use = up if 0 in ds else off
            send([xfer(c, T.s2[:, w * d:w * d + w], T.land[:, mine:mine + w], S["out%d" % me], part(use, len(far), i))
                  for i, (d, c) in enumerate(far)], len(use))

    if rank is not None:
        def arrivals(m):
            d = (rank - 2 * m) % N
            total = 0
            for c in mid[m]:
                for ds in groups:
                    if c != core and d in ds:
                        total += len(up if 0 in ds else off) // len([e for e in ds if T.cores[(2 * m + e) % N] != c])
            return total

        nc = len(mid)
        seq = sorted(range(nc), key=lambda m: [1, 2, 3, 0, 4, 5].index((me - m) % nc))
        for i, m in enumerate(seq):
            q, sem = ((g.sync, S.sty), (g.scalar, S.stz))[i % 2]
            q.wait_ge(S["out%d" % m], arrivals(m))
            if core in mid[m]:
                q.wait_ge(S.own1, 1)
            a, n = start[m], 4 * width[m]
            q.dma_start(T.y[:, a:a + n], T.land[:, a:a + n]).then_inc(sem, 16)
        g.sync.wait_ge(S.sty, 16 * (nc // 2))
        g.scalar.wait_ge(S.stz, 16 * (nc // 2))
    if sent[0]:
        g.wait_ge(S.lsem, sent[0])
